import numpy as np
import ml_dtypes


def mxq(x, axis, fmt="e4m3"):
    dtype, down = {"e4m3": (ml_dtypes.float8_e4m3fn, 7), "e5m2": (ml_dtypes.float8_e5m2, 14)}[fmt]
    v = np.moveaxis(np.asarray(x, np.float32).astype(ml_dtypes.bfloat16).astype(np.float64), axis, -1)
    blocks = v.reshape(v.shape[:-1] + (-1, 32))
    amax = np.abs(blocks).max(-1, keepdims=True)
    byte = np.maximum(np.where(amax > 0, np.frexp(amax)[1] - 1 + 127, 0) - down, 1)
    scale = np.exp2(byte - 127.0)
    codes = (blocks / scale).astype(np.float32).astype(dtype).astype(np.float64)
    return np.moveaxis((codes * scale).reshape(v.shape), -1, axis)


WIDE = False


def mx_kscale(k):
    if not WIDE:
        return np.ones(k)
    levels = np.array([10, -10, 5, -5, 0])
    if k % 512:
        return np.exp2(np.random.permutation(np.resize(levels, k // 32))).repeat(32)
    a = np.empty((k // 512, 16))
    for p in range(k // 512):
        a[p, :8] = np.random.permutation(np.resize(levels, 8))
        for g in range(8):
            far = levels[np.abs(levels - a[p, g]) >= 10]
            a[p, g + 8] = far[np.random.randint(len(far))]
    return np.exp2(a.ravel()).repeat(32)


def f64(x):
    return np.asarray(x).astype(np.float64)


def striped(idx):
    return np.tile(idx.reshape(-1, 16).T, (8, 1)).astype(np.uint16)


def unstriped(offs):
    return offs[:16].T.reshape(-1).astype(np.int64)


def striped8(idx):
    return np.concatenate([x.reshape(-1, 16).T for x in idx]).astype(np.uint16)


def runs(offs, k):
    lists = np.stack([offs[16 * r : 16 * r + 16].T.reshape(-1) for r in range(8)]).astype(np.int64)
    return lists[np.arange(k) % 512 // 64]


def pack_weight(w):
    k, n = w.shape
    w = f64(np.asarray(w, np.float32).astype(ml_dtypes.bfloat16)).reshape(k // 32, 32, n)
    amax = np.abs(w).max(1)
    byte = np.clip(np.where(amax > 0, np.frexp(amax)[1] - 1 + 127 - 7, 1), 1, 254)
    scaled = (w * np.exp2(127.0 - byte)[:, None, :]).reshape(k, n).astype(np.float32)
    words = np.ascontiguousarray(scaled.reshape(k // 512, 128, 4, n).transpose(0, 1, 3, 2)).astype(ml_dtypes.float8_e4m3fn).view(np.uint8)
    return words, np.ascontiguousarray(byte.astype(np.uint8).reshape(k // 512, 16, n))


def unpack_weight(words, scales):
    g, p, n, _ = words.shape
    vals = np.ascontiguousarray(words).view(ml_dtypes.float8_e4m3fn).astype(np.float64) * np.repeat(np.exp2(scales.astype(np.float64) - 127.0), 8, axis=1)[..., None]
    return vals.transpose(0, 1, 3, 2).reshape(g * 512, n)


def relu(v):
    return np.maximum(v, 0.0)

def planes(y):
    n, m = y.shape
    v = y.astype(np.float32).astype(ml_dtypes.bfloat16).astype(np.float64).reshape(n // 32, 32, m)
    top = np.abs(v).max(1)
    byte = np.clip(np.where(top > 0, np.frexp(top)[1] - 1 + 127 - 7, 1), 1, 254)
    codes = (v * np.exp2(127.0 - byte)[:, None, :]).reshape(n, m).astype(np.float32).astype(ml_dtypes.float8_e4m3fn).view(np.uint8)
    words = codes.reshape(n // 512, 128, 4, m).transpose(0, 1, 3, 2)
    return np.ascontiguousarray(words), np.ascontiguousarray(byte.astype(np.uint8).reshape(n // 512, 16, m))


K, T, S, N, H = 512, 2048, 512, 512, 512


def setup_inputs():
    n = np.random.standard_normal
    s = mx_kscale(K)[:, None]
    u = mx_kscale(H)
    packed_xT = pack_weight(n((K, T)) * s)
    packed_w1 = pack_weight(n((K, H)) / np.sqrt(K) / s)
    packed_w2 = pack_weight(n((H, N)) / np.sqrt(H) / u[:, None])
    return {
        "x_words": packed_xT[0],
        "x_scales": packed_xT[1],
        "w1_words": packed_w1[0],
        "w1_scales": packed_w1[1],
        "gn": (np.random.uniform(0.5, 1.5, (H, 1)) * u[:, None]).astype(np.float32),
        "w2_words": packed_w2[0],
        "w2_scales": packed_w2[1],
        "res": (2 * n((N, S))).astype(np.float32),
        "offs": striped(np.random.permutation(T)[:S]),
        "p1": striped8(np.stack([np.random.permutation(S) for _ in range(8)])),
        "p2": striped8(np.stack([np.random.permutation(S) for _ in range(8)])),
    }


def reference(x_words, x_scales, w1_words, w1_scales, gn, w2_words, w2_scales, res, offs, p1, p2):
    xq = unpack_weight(x_words, x_scales)[:, unstriped(offs)]
    y = unpack_weight(w1_words, w1_scales).T @ xq
    ab = np.abs(y)
    env = np.maximum(np.maximum(ab, 0.75 * (ab[np.arange(H)[:, None], runs(p1, H)])), 0.5 * (ab[np.arange(H)[:, None], runs(p2, H)]))
    z = f64(gn) * (y / (relu(env + -0.5) + 1))
    out_0 = f64(res) + (unpack_weight(w2_words, w2_scales).T @ mxq(z, 0, "e4m3"))
    return (out_0,) + planes(out_0)

@@ -1,0 +1,217 @@
+import math
+from contextlib import ExitStack
+
+import concourse.mybir as mybir
+
+K, T, S, N, H = 512, 2048, 512, 512, 512
+FLOPS = 2 * K * H * S + 2 * H * N * S
+
+F32 = mybir.dt.float32
+BF16 = mybir.dt.bfloat16
+I32 = mybir.dt.int32
+U32 = mybir.dt.uint32
+U16 = mybir.dt.uint16
+U8 = mybir.dt.uint8
+FP8X4 = mybir.dt.float8_e4m3fn_x4
+ALU = mybir.AluOpType
+ACT = mybir.ActivationFunctionType
+
+P = 128
+PACK = 4
+QUADS = 4
+HALF = 256
+CHUNK = 128
+TINY = 2.0**-40
+
+
+def tile_picked_compress8_none_po_kernel(
+    tc, x_words, x_scales, w1_words, w1_scales, gn, w2_words, w2_scales, res, offs, p1, p2, out_0, out_1, out_2
+):
+    nc = tc.nc
+    chunks = S // CHUNK
+
+    def as_words(dram):
+        return dram[0].rearrange("p n t -> p (n t)").bitcast(I32)
+
+    def load_scale_rows(queues, plane, dram):
+        for q, queue in enumerate(queues):
+            queue.dma_start(plane[32 * q : 32 * q + 4, :].bitcast(I32), dram[0, 4 * q : 4 * q + 4, :].bitcast(I32))
+
+    def entries(lists, first, count):
+        return lists[:, first // 16 : (first + count) // 16]
+
+    with ExitStack() as ctx:
+        keep = ctx.enter_context(tc.tile_pool(name="keep", bufs=1))
+        psum = ctx.enter_context(tc.psum_pool(name="psum", bufs=1))
+
+        offs_sb = keep.tile([P, S // 16], U16)
+        p1_sb = keep.tile([P, S // 16], U16)
+        p2_sb = keep.tile([P, S // 16], U16)
+        xw = keep.tile([P, T], I32, align_bytes=64, tag="wide")
+        xs = keep.tile([P, T], U8, align_bytes=64, tag="plane")
+        w1w = keep.tile([P, H], I32, align_bytes=64, tag="weights")
+        w1s = keep.tile([P, H], U8, align_bytes=64)
+        gn_sb = keep.tile([P, PACK], F32)
+        half = keep.tile([P, 1], F32)
+
+        nc.vector.memset(xs[:].bitcast(I32), 0)
+        nc.vector.memset(w1s[:].bitcast(I32), 0)
+        nc.vector.memset(half[:], 0.5)
+
+        nc.sync.dma_start(offs_sb[:], offs)
+        nc.sync.dma_start(p1_sb[:], p1)
+        nc.sync.dma_start(p2_sb[:], p2)
+        nc.sync.dma_start(w1w[:], as_words(w1_words))
+        nc.sync.dma_start(xw[:], as_words(x_words))
+        load_scale_rows([nc.scalar] * 4, xs, x_scales)
+        load_scale_rows([nc.gpsimd] + [nc.scalar] * 3, w1s, w1_scales)
+        nc.gpsimd.dma_start(gn_sb[:], gn.rearrange("(p t) o -> p (t o)", t=PACK))
+
+        ln_half = keep.tile([P, 1], F32)
+        nc.scalar.activation(ln_half[:], half[:], ACT.Ln)
+
+        def deal(words, plane, name):
+            dealt_words = keep.tile([P, PACK * P], I32, align_bytes=64, name=name + "_words")
+            dealt_plane = keep.tile([P, PACK * P], U8, align_bytes=64, name=name + "_plane")
+            nc.vector.tensor_copy(
+                dealt_words[:].rearrange("p (t m) -> p t m", t=PACK), words[:].rearrange("p (m t) -> p t m", t=PACK)
+            )
+            nc.vector.tensor_copy(
+                dealt_plane[:].rearrange("p (t m) -> p t m", t=PACK), plane[:].rearrange("p (m t) -> p t m", t=PACK)
+            )
+            return dealt_words, dealt_plane
+
+        picked_s = keep.tile([P, S], U8, align_bytes=64)
+        nc.vector.tensor_copy(picked_s[:], xs[:].indirect(offs_sb[:]))
+        w1d, w1p = deal(w1w, w1s, "w1d")
+
+        w2w = keep.tile([P, N], I32, align_bytes=64, tag="weights")
+        w2s = keep.tile([P, N], U8, align_bytes=64, tag="plane")
+        nc.vector.memset(w2s[:].bitcast(I32), 0)
+        nc.sync.dma_start(w2w[:], as_words(w2_words))
+        load_scale_rows([nc.sync] * 4, w2s, w2_scales)
+
+        y = [psum.tile([P, S], F32, name=f"y{t}") for t in range(PACK)]
+        for h in range(S // HALF):
+            picked_w = keep.tile([P, HALF], U32, align_bytes=64, name=f"picked_w{h}")
+            nc.vector.tensor_copy(picked_w[:], xw[:].bitcast(U32).indirect(entries(offs_sb, h * HALF, HALF)))
+            cols = slice(h * HALF, (h + 1) * HALF)
+            for t in range(PACK):
+                rows = slice(t * P, (t + 1) * P)
+                nc.tensor.matmul_mx(
+                    y[t][:, cols],
+                    lhsT=w1d[:, rows].bitcast(FP8X4),
+                    lhsT_scale=w1p[:, rows],
+                    rhs=picked_w[:].bitcast(FP8X4),
+                    rhs_scale=picked_s[:, cols],
+                    start=True,
+                    stop=True,
+                )
+
+        res_sb = keep.tile([P, PACK, S], F32, align_bytes=64, tag="wide")
+        nc.sync.dma_start(res_sb[:], res.rearrange("(p t) j -> p t j", t=PACK))
+
+        w2d, w2p = deal(w2w, w2s, "w2d")
+        gain2 = keep.tile([P, PACK], F32)
+        nc.vector.tensor_scalar(gain2[:], gn_sb[:], 2.0, None, ALU.mult)
+
+        size = keep.tile([P, PACK, S], F32, tag="scalar_work")
+        logs = [keep.tile([P, S], F32, name=f"logs{t}") for t in range(PACK)]
+        for t in range(PACK):
+            nc.scalar.activation(size[:, t, :], y[t][:], ACT.Abs)
+            nc.scalar.activation(logs[t][:], size[:, t, :], ACT.Ln, bias=TINY)
+
+        near = [keep.tile([P, PACK, HALF], F32, name=f"near{h}") for h in range(S // HALF)]
+        top = [keep.tile([P, PACK, HALF], F32, name=f"top{h}") for h in range(S // HALF)]
+        for h in range(S // HALF):
+            for t in range(PACK):
+                nc.vector.tensor_copy(near[h][:, t, :], logs[t][:].indirect(entries(p1_sb, h * HALF, HALF)))
+            for t in range(PACK):
+                nc.vector.scalar_tensor_tensor(
+                    top[h][:, t, :],
+                    near[h][:, t, :],
+                    math.log(0.75),
+                    logs[t][:, h * HALF : (h + 1) * HALF],
+                    ALU.add,
+                    ALU.max,
+                )
+
+        out_words = keep.tile([P, S], U32, align_bytes=64)
+        out_plane = keep.tile([P, S], U8, align_bytes=64)
+        out_rows = out_0.rearrange("(p t) j -> p t j", t=PACK)
+        out_codes = as_words(out_1)
+
+        def weave(copy, woven, planes):
+            copy(
+                woven[:].rearrange("p (c i t) -> p c t i", i=4, t=PACK),
+                planes[:].rearrange("p t (c i) -> p c t i", i=4),
+            )
+
+        state = {}
+        far_first = keep.tile([P, PACK, CHUNK], F32, tag="scalar_work")
+
+        def top_of(c):
+            h, first = divmod(c * CHUNK, HALF)
+            return top[h][:, :, first : first + CHUNK]
+
+        def factors(c):
+            far = far_first[:] if c == 0 else top_of(c - 1)
+            own = keep.tile([P, PACK, CHUNK], F32, name=f"own{c}")
+            for t in range(PACK):
+                nc.scalar.activation(
+                    far[:, t, :], logs[t][:].indirect(entries(p2_sb, c * CHUNK, CHUNK)), ACT.Sigmoid, scale=-1.0
+                )
+            nc.scalar.activation(own[:], top_of(c), ACT.Sigmoid, bias=ln_half[:], scale=-1.0)
+            least = keep.tile([P, PACK, CHUNK], F32, name=f"least{c}")
+            nc.vector.scalar_tensor_tensor(least[:], own[:], 0.5, far, ALU.min, ALU.min)
+            state[c] = least
+
+        def second_product(c):
+            cols = slice(c * CHUNK, (c + 1) * CHUNK)
+            z = keep.tile([P, PACK, CHUNK], BF16, name=f"z{c}")
+            for t in range(PACK):
+                nc.vector.scalar_tensor_tensor(
+                    z[:, t, :], y[t][:, cols], gain2[:, t : t + 1], state[c][:, t, :], ALU.mult, ALU.mult
+                )
+            z_woven = keep.tile([P, PACK * CHUNK], BF16, align_bytes=64, name=f"z_woven{c}")
+            weave(nc.vector.tensor_copy, z_woven, z)
+            z_words = keep.tile([P, CHUNK], U32, align_bytes=64, name=f"z_words{c}")
+            z_plane = keep.tile([P, CHUNK], U8, align_bytes=64, name=f"z_plane{c}")
+            nc.vector.quantize_mx(z_words[:].bitcast(FP8X4), z_plane[:], z_woven[:])
+            acc = psum.tile([P, PACK, CHUNK], F32, name=f"acc{c}")
+            for t in range(PACK):
+                rows = slice(t * P, (t + 1) * P)
+                nc.tensor.matmul_mx(
+                    acc[:, t, :],
+                    lhsT=w2d[:, rows].bitcast(FP8X4),
+                    lhsT_scale=w2p[:, rows],
+                    rhs=z_words[:].bitcast(FP8X4),
+                    rhs_scale=z_plane[:],
+                    start=True,
+                    stop=True,
+                )
+            state[c] = acc
+
+        def add_residual(c):
+            cols = slice(c * CHUNK, (c + 1) * CHUNK)
+            total = keep.tile([P, PACK, CHUNK], F32, name=f"total{c}")
+            nc.vector.tensor_tensor(total[:], state[c][:], res_sb[:, :, cols], ALU.add)
+            nc.sync.dma_start(out_rows[:, :, cols], total[:])
+            woven = keep.tile([P, PACK * CHUNK], BF16, align_bytes=64, name=f"woven{c}")
+            weave(nc.scalar.copy, woven, total)
+            state[c] = woven
+
+        def hand_on(c):
+            cols = slice(c * CHUNK, (c + 1) * CHUNK)
+            nc.vector.quantize_mx(out_words[:, cols].bitcast(FP8X4), out_plane[:, cols], state[c][:])
+            nc.sync.dma_start(out_codes[:, cols], out_words[:, cols].bitcast(I32))
+
+        stages = (factors, second_product, add_residual, hand_on)
+        for step in range(chunks + len(stages) - 1):
+            for lag, stage in enumerate(stages):
+                if 0 <= step - lag < chunks:
+                    stage(step - lag)
+
+        for q in range(QUADS):
+            queue = nc.sync if q % 2 == 0 else nc.scalar
+            queue.dma_start(out_2[0, 4 * q : 4 * q + 4, :].bitcast(I32), out_plane[32 * q : 32 * q + 4, :].bitcast(I32))

@@ -48,8 +48,10 @@ def tile_picked_compress8_none_po_kernel(
         p1_sb = keep.tile([P, S // 16], U16)
         p2_sb = keep.tile([P, S // 16], U16)
         xw = keep.tile([P, T], I32, align_bytes=64, tag="wide")
-        xs = keep.tile([P, T], U8, align_bytes=64, tag="plane")
-        w1w = keep.tile([P, H], I32, align_bytes=64, tag="weights")
+        xs = keep.tile([P, T], U8, align_bytes=64)
+        w1w = keep.tile([P, H], I32, align_bytes=64)
+        w2w = keep.tile([P, N], I32, align_bytes=64)
+        w2s = keep.tile([P, N], U8, align_bytes=64)
         w1s = keep.tile([P, H], U8, align_bytes=64)
         gn_sb = keep.tile([P, PACK], F32)
         half = keep.tile([P, 1], F32)
@@ -57,79 +59,88 @@ def tile_picked_compress8_none_po_kernel(
         nc.vector.memset(xs[:].bitcast(I32), 0)
         nc.vector.memset(w1s[:].bitcast(I32), 0)
         nc.vector.memset(half[:], 0.5)
+        nc.vector.memset(w2s[:].bitcast(I32), 0)
 
         nc.sync.dma_start(offs_sb[:], offs)
+        load_scale_rows([nc.sync] * 4, xs, x_scales)
         nc.sync.dma_start(p1_sb[:], p1)
         nc.sync.dma_start(p2_sb[:], p2)
         nc.sync.dma_start(w1w[:], as_words(w1_words))
         nc.sync.dma_start(xw[:], as_words(x_words))
-        load_scale_rows([nc.scalar] * 4, xs, x_scales)
-        load_scale_rows([nc.gpsimd] + [nc.scalar] * 3, w1s, w1_scales)
-        nc.gpsimd.dma_start(gn_sb[:], gn.rearrange("(p t) o -> p (t o)", t=PACK))
+        load_scale_rows([nc.sync] * 4, w1s, w1_scales)
+        nc.sync.dma_start(w2w[:], as_words(w2_words))
+        load_scale_rows([nc.sync] * 4, w2s, w2_scales)
+        nc.sync.dma_start(gn_sb[:], gn.rearrange("(p t) o -> p (t o)", t=PACK))
 
         ln_half = keep.tile([P, 1], F32)
         nc.scalar.activation(ln_half[:], half[:], ACT.Ln)
 
-        def deal(words, plane, name):
-            dealt_words = keep.tile([P, PACK * P], I32, align_bytes=64, name=name + "_words")
-            dealt_plane = keep.tile([P, PACK * P], U8, align_bytes=64, name=name + "_plane")
-            nc.vector.tensor_copy(
-                dealt_words[:].rearrange("p (t m) -> p t m", t=PACK), words[:].rearrange("p (m t) -> p t m", t=PACK)
-            )
-            nc.vector.tensor_copy(
-                dealt_plane[:].rearrange("p (t m) -> p t m", t=PACK), plane[:].rearrange("p (m t) -> p t m", t=PACK)
-            )
-            return dealt_words, dealt_plane
+        def by_tile(ap):
+            return ap.rearrange("p (t m) -> p t m", t=PACK)
+
+        def by_residue(ap):
+            return ap.rearrange("p (m t) -> p t m", t=PACK)
 
         picked_s = keep.tile([P, S], U8, align_bytes=64)
         nc.vector.tensor_copy(picked_s[:], xs[:].indirect(offs_sb[:]))
-        w1d, w1p = deal(w1w, w1s, "w1d")
 
-        w2w = keep.tile([P, N], I32, align_bytes=64, tag="weights")
-        w2s = keep.tile([P, N], U8, align_bytes=64, tag="plane")
-        nc.vector.memset(w2s[:].bitcast(I32), 0)
-        nc.sync.dma_start(w2w[:], as_words(w2_words))
-        load_scale_rows([nc.sync] * 4, w2s, w2_scales)
+        picked_w = [keep.tile([P, HALF], U32, align_bytes=64, name=f"picked_w{h}") for h in range(S // HALF)]
+        w1d = keep.tile([P, H], I32, align_bytes=64)
+        w1p = [keep.tile([P, P], U8, align_bytes=64, name=f"w1p{t}") for t in range(PACK)]
+
+        def pick_words(h):
+            nc.vector.tensor_copy(picked_w[h][:], xw[:].bitcast(U32).indirect(entries(offs_sb, h * HALF, HALF)))
+
+        def deal_plane(t):
+            nc.vector.tensor_copy(w1p[t][:], by_residue(w1s[:])[:, t, :])
+
+        pick_words(0)
+        nc.vector.tensor_copy(by_tile(w1d[:]), by_residue(w1w[:]))
+        deal_plane(0)
+        pick_words(1)
+        for t in range(1, PACK):
+            deal_plane(t)
 
         y = [psum.tile([P, S], F32, name=f"y{t}") for t in range(PACK)]
-        for h in range(S // HALF):
-            picked_w = keep.tile([P, HALF], U32, align_bytes=64, name=f"picked_w{h}")
-            nc.vector.tensor_copy(picked_w[:], xw[:].bitcast(U32).indirect(entries(offs_sb, h * HALF, HALF)))
-            cols = slice(h * HALF, (h + 1) * HALF)
-            for t in range(PACK):
-                rows = slice(t * P, (t + 1) * P)
+        for t in range(PACK):
+            for h in range(S // HALF):
+                cols = slice(h * HALF, (h + 1) * HALF)
                 nc.tensor.matmul_mx(
                     y[t][:, cols],
-                    lhsT=w1d[:, rows].bitcast(FP8X4),
-                    lhsT_scale=w1p[:, rows],
-                    rhs=picked_w[:].bitcast(FP8X4),
+                    lhsT=w1d[:, t * P : (t + 1) * P].bitcast(FP8X4),
+                    lhsT_scale=w1p[t][:],
+                    rhs=picked_w[h][:].bitcast(FP8X4),
                     rhs_scale=picked_s[:, cols],
                     start=True,
                     stop=True,
                 )
 
+        w2d = keep.tile([P, N], I32, align_bytes=64)
+        w2p = keep.tile([P, N], U8, align_bytes=64)
+        nc.vector.tensor_copy(by_tile(w2d[:]), by_residue(w2w[:]))
+        nc.vector.tensor_copy(by_tile(w2p[:]), by_residue(w2s[:]))
+
         res_sb = keep.tile([P, PACK, S], F32, align_bytes=64, tag="wide")
         nc.sync.dma_start(res_sb[:], res.rearrange("(p t) j -> p t j", t=PACK))
 
-        w2d, w2p = deal(w2w, w2s, "w2d")
         gain2 = keep.tile([P, PACK], F32)
         nc.vector.tensor_scalar(gain2[:], gn_sb[:], 2.0, None, ALU.mult)
 
-        size = keep.tile([P, PACK, S], F32, tag="scalar_work")
+        size = [keep.tile([P, S], F32, align_bytes=64, name=f"size{t}", tag=f"size{t}") for t in range(PACK)]
         logs = [keep.tile([P, S], F32, name=f"logs{t}") for t in range(PACK)]
         for t in range(PACK):
-            nc.scalar.activation(size[:, t, :], y[t][:], ACT.Abs)
-            nc.scalar.activation(logs[t][:], size[:, t, :], ACT.Ln, bias=TINY)
+            nc.scalar.activation(size[t][:], y[t][:], ACT.Abs)
+            nc.scalar.activation(logs[t][:], size[t][:], ACT.Ln, bias=TINY)
 
-        near = [keep.tile([P, PACK, HALF], F32, name=f"near{h}") for h in range(S // HALF)]
         top = [keep.tile([P, PACK, HALF], F32, name=f"top{h}") for h in range(S // HALF)]
         for h in range(S // HALF):
+            near = keep.tile([P, PACK, HALF], F32, name=f"near{h}")
             for t in range(PACK):
-                nc.vector.tensor_copy(near[h][:, t, :], logs[t][:].indirect(entries(p1_sb, h * HALF, HALF)))
+                nc.vector.tensor_copy(near[:, t, :], logs[t][:].indirect(entries(p1_sb, h * HALF, HALF)))
             for t in range(PACK):
                 nc.vector.scalar_tensor_tensor(
                     top[h][:, t, :],
-                    near[h][:, t, :],
+                    near[:, t, :],
                     math.log(0.75),
                     logs[t][:, h * HALF : (h + 1) * HALF],
                     ALU.add,
@@ -148,7 +159,7 @@ def tile_picked_compress8_none_po_kernel(
             )
 
         state = {}
-        far_first = keep.tile([P, PACK, CHUNK], F32, tag="scalar_work")
+        far_first = keep.tile([P, PACK, CHUNK], F32, align_bytes=64, tag="size3")
 
         def top_of(c):
             h, first = divmod(c * CHUNK, HALF)
@@ -174,7 +185,7 @@ def tile_picked_compress8_none_po_kernel(
                     z[:, t, :], y[t][:, cols], gain2[:, t : t + 1], state[c][:, t, :], ALU.mult, ALU.mult
                 )
             z_woven = keep.tile([P, PACK * CHUNK], BF16, align_bytes=64, name=f"z_woven{c}")
-            weave(nc.vector.tensor_copy, z_woven, z)
+            weave(nc.scalar.copy if c < chunks - 1 else nc.vector.tensor_copy, z_woven, z)
             z_words = keep.tile([P, CHUNK], U32, align_bytes=64, name=f"z_words{c}")
             z_plane = keep.tile([P, CHUNK], U8, align_bytes=64, name=f"z_plane{c}")
             nc.vector.quantize_mx(z_words[:].bitcast(FP8X4), z_plane[:], z_woven[:])
@@ -198,7 +209,7 @@ def tile_picked_compress8_none_po_kernel(
             nc.vector.tensor_tensor(total[:], state[c][:], res_sb[:, :, cols], ALU.add)
             nc.sync.dma_start(out_rows[:, :, cols], total[:])
             woven = keep.tile([P, PACK * CHUNK], BF16, align_bytes=64, name=f"woven{c}")
-            weave(nc.scalar.copy, woven, total)
+            weave(nc.scalar.copy if c < chunks - 1 else nc.vector.tensor_copy, woven, total)
             state[c] = woven
 
         def hand_on(c):
@@ -208,7 +219,7 @@ def tile_picked_compress8_none_po_kernel(
 
         stages = (factors, second_product, add_residual, hand_on)
         for step in range(chunks + len(stages) - 1):
-            for lag, stage in enumerate(stages):
+            for lag, stage in reversed(list(enumerate(stages))):
                 if 0 <= step - lag < chunks:
                     stage(step - lag)
 

@@ -21,6 +21,8 @@ PACK = 4
 QUADS = 4
 HALF = 256
 CHUNK = 128
+PIECES = (128, 128, 128, 128)
+Z_ON_SCALAR = (2, 3)
 TINY = 2.0**-40
 
 
@@ -129,18 +131,23 @@ def tile_picked_compress8_none_po_kernel(
         size = [keep.tile([P, S], F32, align_bytes=64, name=f"size{t}", tag=f"size{t}") for t in range(PACK)]
         logs = [keep.tile([P, S], F32, name=f"logs{t}") for t in range(PACK)]
         for t in range(PACK):
-            nc.scalar.activation(size[t][:], y[t][:], ACT.Abs)
-            nc.scalar.activation(logs[t][:], size[t][:], ACT.Ln, bias=TINY)
+            for h in range(S // HALF):
+                cols = slice(h * HALF, (h + 1) * HALF)
+                nc.scalar.activation(size[t][:, cols], y[t][:, cols], ACT.Abs)
+            for h in range(S // HALF):
+                cols = slice(h * HALF, (h + 1) * HALF)
+                nc.scalar.activation(logs[t][:, cols], size[t][:, cols], ACT.Ln, bias=TINY)
 
+        near = keep.tile([P, 6, HALF], F32)
         top = [keep.tile([P, PACK, HALF], F32, name=f"top{h}") for h in range(S // HALF)]
         for h in range(S // HALF):
-            near = keep.tile([P, PACK, HALF], F32, name=f"near{h}")
+            rows = [near[:, t if h == 0 else (4, 5, 3, 2)[t], :] for t in range(PACK)]
             for t in range(PACK):
-                nc.vector.tensor_copy(near[:, t, :], logs[t][:].indirect(entries(p1_sb, h * HALF, HALF)))
+                nc.vector.tensor_copy(rows[t], logs[t][:].indirect(entries(p1_sb, h * HALF, HALF)))
             for t in range(PACK):
                 nc.vector.scalar_tensor_tensor(
                     top[h][:, t, :],
-                    near[:, t, :],
+                    rows[t],
                     math.log(0.75),
                     logs[t][:, h * HALF : (h + 1) * HALF],
                     ALU.add,
@@ -165,31 +172,36 @@ def tile_picked_compress8_none_po_kernel(
             h, first = divmod(c * CHUNK, HALF)
             return top[h][:, :, first : first + CHUNK]
 
-        def factors(c):
-            far = far_first[:] if c == 0 else top_of(c - 1)
-            own = keep.tile([P, PACK, CHUNK], F32, name=f"own{c}")
+        far, own = [], []
+        for c in range(chunks):
+            far.append(far_first[:] if c == 0 else top_of(c - 1))
+            own.append(keep.tile([P, PACK, CHUNK], F32, name=f"own{c}"))
             for t in range(PACK):
                 nc.scalar.activation(
-                    far[:, t, :], logs[t][:].indirect(entries(p2_sb, c * CHUNK, CHUNK)), ACT.Sigmoid, scale=-1.0
+                    far[c][:, t, :], logs[t][:].indirect(entries(p2_sb, c * CHUNK, CHUNK)), ACT.Sigmoid, scale=-1.0
                 )
-            nc.scalar.activation(own[:], top_of(c), ACT.Sigmoid, bias=ln_half[:], scale=-1.0)
-            least = keep.tile([P, PACK, CHUNK], F32, name=f"least{c}")
-            nc.vector.scalar_tensor_tensor(least[:], own[:], 0.5, far, ALU.min, ALU.min)
-            state[c] = least
+            nc.scalar.activation(own[c][:], top_of(c), ACT.Sigmoid, bias=ln_half[:], scale=-1.0)
 
-        def second_product(c):
-            cols = slice(c * CHUNK, (c + 1) * CHUNK)
-            z = keep.tile([P, PACK, CHUNK], BF16, name=f"z{c}")
+        starts = [sum(PIECES[:i]) for i in range(len(PIECES))]
+
+        def second_product(i):
+            first, width = starts[i], PIECES[i]
+            cols = slice(first, first + width)
+            c, inner = divmod(first, CHUNK)
+            part = slice(inner, inner + width)
+            least = keep.tile([P, PACK, width], F32, name=f"least{i}")
+            nc.vector.scalar_tensor_tensor(least[:], own[c][:, :, part], 0.5, far[c][:, :, part], ALU.min, ALU.min)
+            z = keep.tile([P, PACK, width], BF16, name=f"z{i}")
             for t in range(PACK):
                 nc.vector.scalar_tensor_tensor(
-                    z[:, t, :], y[t][:, cols], gain2[:, t : t + 1], state[c][:, t, :], ALU.mult, ALU.mult
+                    z[:, t, :], y[t][:, cols], gain2[:, t : t + 1], least[:, t, :], ALU.mult, ALU.mult
                 )
-            z_woven = keep.tile([P, PACK * CHUNK], BF16, align_bytes=64, name=f"z_woven{c}")
-            weave(nc.scalar.copy if c < chunks - 1 else nc.vector.tensor_copy, z_woven, z)
-            z_words = keep.tile([P, CHUNK], U32, align_bytes=64, name=f"z_words{c}")
-            z_plane = keep.tile([P, CHUNK], U8, align_bytes=64, name=f"z_plane{c}")
+            z_woven = keep.tile([P, PACK * width], BF16, align_bytes=64, name=f"z_woven{i}")
+            weave(nc.scalar.copy if i in Z_ON_SCALAR else nc.vector.tensor_copy, z_woven, z)
+            z_words = keep.tile([P, width], U32, align_bytes=64, name=f"z_words{i}")
+            z_plane = keep.tile([P, width], U8, align_bytes=64, name=f"z_plane{i}")
             nc.vector.quantize_mx(z_words[:].bitcast(FP8X4), z_plane[:], z_woven[:])
-            acc = psum.tile([P, PACK, CHUNK], F32, name=f"acc{c}")
+            acc = psum.tile([P, PACK, width], F32, name="acc", bufs=4)
             for t in range(PACK):
                 rows = slice(t * P, (t + 1) * P)
                 nc.tensor.matmul_mx(
@@ -201,26 +213,27 @@ def tile_picked_compress8_none_po_kernel(
                     start=True,
                     stop=True,
                 )
-            state[c] = acc
+            state[i] = acc
 
-        def add_residual(c):
-            cols = slice(c * CHUNK, (c + 1) * CHUNK)
-            total = keep.tile([P, PACK, CHUNK], F32, name=f"total{c}")
-            nc.vector.tensor_tensor(total[:], state[c][:], res_sb[:, :, cols], ALU.add)
+        def add_residual(i):
+            first, width = starts[i], PIECES[i]
+            cols = slice(first, first + width)
+            total = keep.tile([P, PACK, width], F32, name=f"total{i}")
+            nc.vector.tensor_tensor(total[:], state[i][:], res_sb[:, :, cols], ALU.add)
             nc.sync.dma_start(out_rows[:, :, cols], total[:])
-            woven = keep.tile([P, PACK * CHUNK], BF16, align_bytes=64, name=f"woven{c}")
-            weave(nc.scalar.copy if c < chunks - 1 else nc.vector.tensor_copy, woven, total)
-            state[c] = woven
+            woven = keep.tile([P, PACK * width], BF16, align_bytes=64, name=f"woven{i}")
+            weave(nc.scalar.copy if i < len(PIECES) - 1 else nc.vector.tensor_copy, woven, total)
+            state[i] = woven
 
-        def hand_on(c):
-            cols = slice(c * CHUNK, (c + 1) * CHUNK)
-            nc.vector.quantize_mx(out_words[:, cols].bitcast(FP8X4), out_plane[:, cols], state[c][:])
+        def hand_on(i):
+            cols = slice(starts[i], starts[i] + PIECES[i])
+            nc.vector.quantize_mx(out_words[:, cols].bitcast(FP8X4), out_plane[:, cols], state[i][:])
             nc.sync.dma_start(out_codes[:, cols], out_words[:, cols].bitcast(I32))
 
-        stages = (factors, second_product, add_residual, hand_on)
-        for step in range(chunks + len(stages) - 1):
-            for lag, stage in reversed(list(enumerate(stages))):
-                if 0 <= step - lag < chunks:
+        stages = ((3, hand_on), (1, add_residual), (0, second_product))
+        for step in range(len(PIECES) + 3):
+            for lag, stage in stages:
+                if 0 <= step - lag < len(PIECES):
                     stage(step - lag)
 
         for q in range(QUADS):

import math
from contextlib import ExitStack

import concourse.mybir as mybir

K, T, S, N, H = 512, 2048, 512, 512, 512
FLOPS = 2 * K * H * S + 2 * H * N * S

F32 = mybir.dt.float32
BF16 = mybir.dt.bfloat16
I32 = mybir.dt.int32
U32 = mybir.dt.uint32
U16 = mybir.dt.uint16
U8 = mybir.dt.uint8
FP8X4 = mybir.dt.float8_e4m3fn_x4
ALU = mybir.AluOpType
ACT = mybir.ActivationFunctionType

P = 128
PACK = 4
QUADS = 4
HALF = 256
CHUNK = 128
PIECES = (128, 128, 128, 128)
Z_ON_SCALAR = (2, 3)
TINY = 2.0**-40


def tile_picked_compress8_none_po_kernel(
    tc, x_words, x_scales, w1_words, w1_scales, gn, w2_words, w2_scales, res, offs, p1, p2, out_0, out_1, out_2
):
    nc = tc.nc
    chunks = S // CHUNK

    def as_words(dram):
        return dram[0].rearrange("p n t -> p (n t)").bitcast(I32)

    def load_scale_rows(queues, plane, dram):
        for q, queue in enumerate(queues):
            queue.dma_start(plane[32 * q : 32 * q + 4, :].bitcast(I32), dram[0, 4 * q : 4 * q + 4, :].bitcast(I32))

    def entries(lists, first, count):
        return lists[:, first // 16 : (first + count) // 16]

    with ExitStack() as ctx:
        keep = ctx.enter_context(tc.tile_pool(name="keep", bufs=1))
        psum = ctx.enter_context(tc.psum_pool(name="psum", bufs=1))

        offs_sb = keep.tile([P, S // 16], U16)
        p1_sb = keep.tile([P, S // 16], U16)
        p2_sb = keep.tile([P, S // 16], U16)
        xw = keep.tile([P, T], I32, align_bytes=64, tag="wide")
        xs = keep.tile([P, T], U8, align_bytes=64)
        w1w = keep.tile([P, H], I32, align_bytes=64)
        w2w = keep.tile([P, N], I32, align_bytes=64)
        w2s = keep.tile([P, N], U8, align_bytes=64)
        w1s = keep.tile([P, H], U8, align_bytes=64)
        gn_sb = keep.tile([P, PACK], F32)
        half = keep.tile([P, 1], F32)

        nc.vector.memset(xs[:].bitcast(I32), 0)
        nc.vector.memset(w1s[:].bitcast(I32), 0)
        nc.vector.memset(half[:], 0.5)
        nc.vector.memset(w2s[:].bitcast(I32), 0)

        nc.sync.dma_start(offs_sb[:], offs)
        load_scale_rows([nc.sync] * 4, xs, x_scales)
        nc.sync.dma_start(p1_sb[:], p1)
        nc.sync.dma_start(p2_sb[:], p2)
        nc.sync.dma_start(w1w[:], as_words(w1_words))
        nc.sync.dma_start(xw[:], as_words(x_words))
        load_scale_rows([nc.sync] * 4, w1s, w1_scales)
        nc.sync.dma_start(w2w[:], as_words(w2_words))
        load_scale_rows([nc.sync] * 4, w2s, w2_scales)
        nc.sync.dma_start(gn_sb[:], gn.rearrange("(p t) o -> p (t o)", t=PACK))

        ln_half = keep.tile([P, 1], F32)
        nc.scalar.activation(ln_half[:], half[:], ACT.Ln)

        def by_tile(ap):
            return ap.rearrange("p (t m) -> p t m", t=PACK)

        def by_residue(ap):
            return ap.rearrange("p (m t) -> p t m", t=PACK)

        picked_s = keep.tile([P, S], U8, align_bytes=64)
        nc.vector.tensor_copy(picked_s[:], xs[:].indirect(offs_sb[:]))

        picked_w = [keep.tile([P, HALF], U32, align_bytes=64, name=f"picked_w{h}") for h in range(S // HALF)]
        w1d = keep.tile([P, H], I32, align_bytes=64)
        w1p = [keep.tile([P, P], U8, align_bytes=64, name=f"w1p{t}") for t in range(PACK)]

        def pick_words(h):
            nc.vector.tensor_copy(picked_w[h][:], xw[:].bitcast(U32).indirect(entries(offs_sb, h * HALF, HALF)))

        def deal_plane(t):
            nc.vector.tensor_copy(w1p[t][:], by_residue(w1s[:])[:, t, :])

        pick_words(0)
        nc.vector.tensor_copy(by_tile(w1d[:]), by_residue(w1w[:]))
        deal_plane(0)
        pick_words(1)
        for t in range(1, PACK):
            deal_plane(t)

        y = [psum.tile([P, S], F32, name=f"y{t}") for t in range(PACK)]
        for t in range(PACK):
            for h in range(S // HALF):
                cols = slice(h * HALF, (h + 1) * HALF)
                nc.tensor.matmul_mx(
                    y[t][:, cols],
                    lhsT=w1d[:, t * P : (t + 1) * P].bitcast(FP8X4),
                    lhsT_scale=w1p[t][:],
                    rhs=picked_w[h][:].bitcast(FP8X4),
                    rhs_scale=picked_s[:, cols],
                    start=True,
                    stop=True,
                )

        w2d = keep.tile([P, N], I32, align_bytes=64)
        w2p = keep.tile([P, N], U8, align_bytes=64)
        nc.vector.tensor_copy(by_tile(w2d[:]), by_residue(w2w[:]))
        nc.vector.tensor_copy(by_tile(w2p[:]), by_residue(w2s[:]))

        res_sb = keep.tile([P, PACK, S], F32, align_bytes=64, tag="wide")
        nc.sync.dma_start(res_sb[:], res.rearrange("(p t) j -> p t j", t=PACK))

        gain2 = keep.tile([P, PACK], F32)
        nc.vector.tensor_scalar(gain2[:], gn_sb[:], 2.0, None, ALU.mult)

        size = [keep.tile([P, S], F32, align_bytes=64, name=f"size{t}", tag=f"size{t}") for t in range(PACK)]
        logs = [keep.tile([P, S], F32, name=f"logs{t}") for t in range(PACK)]
        for t in range(PACK):
            for h in range(S // HALF):
                cols = slice(h * HALF, (h + 1) * HALF)
                nc.scalar.activation(size[t][:, cols], y[t][:, cols], ACT.Abs)
            for h in range(S // HALF):
                cols = slice(h * HALF, (h + 1) * HALF)
                nc.scalar.activation(logs[t][:, cols], size[t][:, cols], ACT.Ln, bias=TINY)

        near = keep.tile([P, 6, HALF], F32)
        top = [keep.tile([P, PACK, HALF], F32, name=f"top{h}") for h in range(S // HALF)]
        for h in range(S // HALF):
            rows = [near[:, t if h == 0 else (4, 5, 3, 2)[t], :] for t in range(PACK)]
            for t in range(PACK):
                nc.vector.tensor_copy(rows[t], logs[t][:].indirect(entries(p1_sb, h * HALF, HALF)))
            for t in range(PACK):
                nc.vector.scalar_tensor_tensor(
                    top[h][:, t, :],
                    rows[t],
                    math.log(0.75),
                    logs[t][:, h * HALF : (h + 1) * HALF],
                    ALU.add,
                    ALU.max,
                )

        out_words = keep.tile([P, S], U32, align_bytes=64)
        out_plane = keep.tile([P, S], U8, align_bytes=64)
        out_rows = out_0.rearrange("(p t) j -> p t j", t=PACK)
        out_codes = as_words(out_1)

        def weave(copy, woven, planes):
            copy(
                woven[:].rearrange("p (c i t) -> p c t i", i=4, t=PACK),
                planes[:].rearrange("p t (c i) -> p c t i", i=4),
            )

        state = {}
        far_first = keep.tile([P, PACK, CHUNK], F32, align_bytes=64, tag="size3")

        def top_of(c):
            h, first = divmod(c * CHUNK, HALF)
            return top[h][:, :, first : first + CHUNK]

        far, own = [], []
        for c in range(chunks):
            far.append(far_first[:] if c == 0 else top_of(c - 1))
            own.append(keep.tile([P, PACK, CHUNK], F32, name=f"own{c}"))
            for t in range(PACK):
                nc.scalar.activation(
                    far[c][:, t, :], logs[t][:].indirect(entries(p2_sb, c * CHUNK, CHUNK)), ACT.Sigmoid, scale=-1.0
                )
            nc.scalar.activation(own[c][:], top_of(c), ACT.Sigmoid, bias=ln_half[:], scale=-1.0)

        starts = [sum(PIECES[:i]) for i in range(len(PIECES))]

        def second_product(i):
            first, width = starts[i], PIECES[i]
            cols = slice(first, first + width)
            c, inner = divmod(first, CHUNK)
            part = slice(inner, inner + width)
            least = keep.tile([P, PACK, width], F32, name=f"least{i}")
            nc.vector.scalar_tensor_tensor(least[:], own[c][:, :, part], 0.5, far[c][:, :, part], ALU.min, ALU.min)
            z = keep.tile([P, PACK, width], BF16, name=f"z{i}")
            for t in range(PACK):
                nc.vector.scalar_tensor_tensor(
                    z[:, t, :], y[t][:, cols], gain2[:, t : t + 1], least[:, t, :], ALU.mult, ALU.mult
                )
            z_woven = keep.tile([P, PACK * width], BF16, align_bytes=64, name=f"z_woven{i}")
            weave(nc.scalar.copy if i in Z_ON_SCALAR else nc.vector.tensor_copy, z_woven, z)
            z_words = keep.tile([P, width], U32, align_bytes=64, name=f"z_words{i}")
            z_plane = keep.tile([P, width], U8, align_bytes=64, name=f"z_plane{i}")
            nc.vector.quantize_mx(z_words[:].bitcast(FP8X4), z_plane[:], z_woven[:])
            acc = psum.tile([P, PACK, width], F32, name="acc", bufs=4)
            for t in range(PACK):
                rows = slice(t * P, (t + 1) * P)
                nc.tensor.matmul_mx(
                    acc[:, t, :],
                    lhsT=w2d[:, rows].bitcast(FP8X4),
                    lhsT_scale=w2p[:, rows],
                    rhs=z_words[:].bitcast(FP8X4),
                    rhs_scale=z_plane[:],
                    start=True,
                    stop=True,
                )
            state[i] = acc

        def add_residual(i):
            first, width = starts[i], PIECES[i]
            cols = slice(first, first + width)
            total = keep.tile([P, PACK, width], F32, name=f"total{i}")
            nc.vector.tensor_tensor(total[:], state[i][:], res_sb[:, :, cols], ALU.add)
            nc.sync.dma_start(out_rows[:, :, cols], total[:])
            woven = keep.tile([P, PACK * width], BF16, align_bytes=64, name=f"woven{i}")
            weave(nc.scalar.copy if i < len(PIECES) - 1 else nc.vector.tensor_copy, woven, total)
            state[i] = woven

        def hand_on(i):
            cols = slice(starts[i], starts[i] + PIECES[i])
            nc.vector.quantize_mx(out_words[:, cols].bitcast(FP8X4), out_plane[:, cols], state[i][:])
            nc.sync.dma_start(out_codes[:, cols], out_words[:, cols].bitcast(I32))

        stages = ((3, hand_on), (1, add_residual), (0, second_product))
        for step in range(len(PIECES) + 3):
            for lag, stage in stages:
                if 0 <= step - lag < len(PIECES):
                    stage(step - lag)

        for q in range(QUADS):
            queue = nc.sync if q % 2 == 0 else nc.scalar
            queue.dma_start(out_2[0, 4 * q : 4 * q + 4, :].bitcast(I32), out_plane[32 * q : 32 * q + 4, :].bitcast(I32))
